import numpy as np, ml_dtypes
CORES = [24,25,26,27,28,29,30,31]
N = 8
BF = ml_dtypes.bfloat16
def f(rng, *shape):
    return (rng.standard_normal(shape, dtype=np.float32) * np.exp2(rng.integers(-2, 3, shape[:-1] + (1,)))).astype(BF)
def wide(rng, *shape):
    v = f(rng, *shape).astype(np.float32); k = shape[:-2] + (1, shape[-1])
    return (v * np.exp2(rng.integers(-6, 7, k)) * (rng.random(k) > 0.0625)).astype(BF)
def gentries(a):
    return np.ascontiguousarray(a.reshape(8, 16, -1).transpose(0, 2, 1)).reshape(8, -1)
def gtable(e):
    e = np.asarray(e); return np.ascontiguousarray(e.reshape(8, -1, 16).transpose(0, 2, 1)).reshape(128, -1).astype(np.int32)
L, K, R, D = 8192, 256, 5, 4095
def corner(rng):
    return rng.integers(0, 4096 - D, (2, 1, 8, 1))
def walk(rng):
    v = np.repeat(rng.integers(-3, 4, (N, 8, L // 64)), 64, axis=2) + rng.integers(-1, 2, (N, 8, L))
    m = (rng.integers(0, D + 1, (N, 8, 1)) + np.add.accumulate(v, axis=2)) % (2 * D)
    return D - np.abs(m - D)
def listeners(rng, o):
    return rng.integers(D, L - 1, (N, 8, K)), o[0] + rng.integers(0, D + 1, (N, 8, K)), o[1] + rng.integers(0, D + 1, (N, 8, K))
def packed(X, Y, s, t, x, z):
    return {"track": (X * 4096 + Y).astype(np.int32), "sound": s, "when": np.stack([gtable(a) for a in t]), "place": np.stack([gtable(a) for a in x * 4096 + z])}
def setup_inputs(rng):
    o = corner(rng); t, x, z = listeners(rng, o)
    return packed(o[0] + walk(rng), o[1] + walk(rng), f(rng, N, 128, L), t, x, z)
def setup_inputs_ends(rng):
    o = np.zeros((2, 1, 8, 1), np.int64); o[:, :, 1::2] = 4095 - D
    X, Y = o[0] + walk(rng), o[1] + walk(rng); t, x, z = listeners(rng, o)
    for g in range(8):
        q = int(rng.integers(0, N)); c = int(o[0, 0, g, 0]); near, far = (c, c + D) if g % 2 == 0 else (c + D, c)
        X[q, g, :D + 1] = near; Y[q, g, :D + 1] = near
        t[:, g, 0] = D; x[:, g, 0] = far; z[:, g, 0] = far
        for r in range(N):
            p = (r + 1) % N; t[r, g, K - 1] = L - 2; x[r, g, K - 1] = X[p, g, L - 2]; z[r, g, K - 1] = Y[p, g, L - 2]
    return packed(X, Y, f(rng, N, 128, L), t, x, z)
def setup_inputs_jumps(rng):
    o = corner(rng); t, x, z = listeners(rng, o)
    return packed(o[0] + rng.integers(0, D + 1, (N, 8, L)), o[1] + rng.integers(0, D + 1, (N, 8, L)), f(rng, N, 128, L), t, x, z)
def setup_inputs_still(rng):
    o = corner(rng); t, x, z = listeners(rng, o); X, Y = o[0] + walk(rng), o[1] + walk(rng)
    q = int(rng.integers(0, N)); r = (q + 1) % N; w = (q + 2) % N
    X[q] = X[q, :, :1].copy(); Y[q] = Y[q, :, :1].copy()
    for a in (t, x, z): a[r, :4] = a[r, :4, :1].copy()
    t[w] = np.sort(t[w], axis=1); x[w] = x[w, :, :1].copy(); z[w] = z[w, :, :1].copy()
    return packed(X, Y, f(rng, N, 128, L), t, x, z)
def setup_inputs_sizes(rng):
    d = np.array([0, 4094, 3, 4000, 64, 3000, 500, 2049]).reshape(1, 8, 1)
    o = rng.integers(0, 4096 - d, (2, 1, 8, 1))
    h = lambda n: rng.integers(0, d + 1, (N, 8, n))
    t = rng.integers(d, L - 1, (N, 8, K)); t[:, 0, 0] = 0
    return packed(o[0] + h(L), o[1] + h(L), f(rng, N, 128, L), t, o[0] + h(K), o[1] + h(K))
def setup_inputs_spread(rng):
    d = setup_inputs(rng); d["sound"] = wide(rng, N, 128, L); return d
def check_inputs(d):
    bad = []; tr = np.asarray(d["track"]).astype(np.int64); pl = np.asarray(d["place"]).astype(np.int64); wh = np.asarray(d["when"]).astype(np.int64)
    if not np.isfinite(np.asarray(d["sound"]).astype(np.float32)).all(): bad.append("finite")
    if tr.min() < 0 or tr.max() >= 4096 * 4096: bad.append("track")
    if pl.min() < 0 or pl.max() >= 4096 * 4096: bad.append("place")
    if wh.min() < 0 or wh.max() > L - 2: bad.append("when")
    ok = True
    for r in range(N):
        t = gentries(wh[r]); w = gentries(pl[r])
        for q in range(N):
            e = np.clip(t, 0, L - 2)
            for i in range(R):
                v = np.take_along_axis(tr[q], e, 1)
                e = t - np.maximum(np.abs((v >> 12) - (w >> 12)), np.abs((v & 4095) - (w & 4095)))
                ok = ok and bool(e.min() >= 0) and bool(e.max() <= L - 2); e = np.clip(e, 0, L - 2)
    if not ok: bad.append("inside")
    return bad
def reference(track, sound, when, place):
    y = np.zeros((N, 128, K), np.float32); s = sound.astype(np.float32).reshape(N, 8, 16, L); tr = track.astype(np.int64)
    for r in range(N):
        t = gentries(when[r]).astype(np.int64); w = gentries(place[r]).astype(np.int64)
        for q in range(N):
            e = t
            for i in range(R):
                v = np.take_along_axis(tr[q], e, 1)
                e = t - np.maximum(np.abs((v >> 12) - (w >> 12)), np.abs((v & 4095) - (w & 4095)))
            u = np.take_along_axis(s[q], e[:, None, :], 2) + np.take_along_axis(s[q], e[:, None, :] + 1, 2)
            y[r] += u.astype(BF).astype(np.float32).reshape(128, K)
    return {"y": y}

@@ -1,0 +1,347 @@
+from concourse.bass import DstId, RemoteDMATransfer
+from concourse.mybir import AluOpType, ActivationFunctionType
+
+N = 8
+R = 5
+L = 8192
+ZV, ZS = 5632, 512
+VW = 32
+VM = 20
+VF = 32
+UP = [0, 1, 1, 1, 1, 0, 0]
+H = 512 * sum(UP)
+CUT = 1024
+MID = 5632
+NA = 6
+SCRATCH = {
+    "land": ("sbuf", [128, 8, 32], "int32"),
+    "pxy": ("sbuf", [128, 2, 8, 16], "int32"),
+    "cx": ("sbuf", [128, 2, 8, 32], "float16"),
+    "tf": ("sbuf", [128, 8, 16], "float32"),
+    "win": ("sbuf", [128, L], "bfloat16"),
+    "snd": ("sbuf", [128, 4608], "bfloat16"),
+    "us": ("sbuf", [128, L], "bfloat16"),
+    "trk": ("sbuf", [128, 512], "int32"),
+    "dig": ("sbuf", [128, 4, 512], "int32"),
+    "dgb": ("sbuf", [128, 4, 512], "bfloat16"),
+    "v0": ("sbuf", [128, 1024], "bfloat16"),
+    "v1": ("sbuf", [128, 1024], "bfloat16"),
+    "u0": ("sbuf", [128, 1024], "bfloat16"),
+    "u1": ("sbuf", [128, 1024], "bfloat16"),
+    "a0": ("sbuf", [128, 16, 16], "float32"),
+    "a1": ("sbuf", [128, 16, 16], "float32"),
+    "l0": ("sbuf", [128, 64], "uint16"),
+    "l1": ("sbuf", [128, 64], "uint16"),
+    "ul": ("sbuf", [128, 8, 256], "bfloat16"),
+    "ysb": ("sbuf", [128, 256], "float32"),
+    "zb": ("sbuf", [128, 128], "bfloat16"),
+    "i1": ("sbuf", [128, 128], "bfloat16"),
+    "i32": ("sbuf", [128, 128], "float32"),
+    "ec": ("sbuf", [128, 4, 8], "bfloat16"),
+    "es": ("sbuf", [128, 2, 8], "bfloat16"),
+    "r16": ("sbuf", [128, 16], "bfloat16"),
+    "qb": ("sbuf", [128, 2, 2, 32], "bfloat16"),
+    "qn": ("sbuf", [128, 2, 2, 2, 32], "float16"),
+    "rb": ("sbuf", [128, 2, 64], "bfloat16"),
+    "rm": ("sbuf", [128, 64], "float32"),
+    "pi": ("sbuf", [128, 8], "int32"),
+    "mki": ("sbuf", [128, 8], "int32"),
+    "mkf": ("sbuf", [128, 8], "float32"),
+    "p00": ("psum", [128, 128, 4], "float32"),
+    "p01": ("psum", [128, 128, 4], "float32"),
+    "p10": ("psum", [128, 128, 4], "float32"),
+    "p11": ("psum", [128, 128, 4], "float32"),
+    "q0": ("psum", [128, 512], "float32"),
+    "q1": ("psum", [128, 512], "float32"),
+    "w0": ("psum", [128, 512], "float32"),
+    "w1": ("psum", [128, 512], "float32"),
+}
+SEMAPHORES = (["vz", "vy", "gi", "ge", "gq", "gm", "g1", "vb", "vm", "dl", "dt", "vp0", "vp1", "vk", "ve", "vn", "vw", "sz", "dw",
+               "arr", "ls", "lu", "yp0", "yp1", "yc0", "yc1", "dy0", "dy1", "dn0", "dn1", "dn2", "dn3", "ga0", "ga1", "pu", "vu"]
+              + ["vd%d" % c for c in range(4)] + ["sd%d" % c for c in range(4)]
+              + ["%s%d" % (k, x) for k in ("gv", "gs", "st", "ab", "tr", "cp", "fv", "fs") for x in range(2)]
+              + ["uq%d" % q for q in range(N)])
+CALLS = [(0, 1, 2, 3), (4, 5), (6,)]
+WIDTH = [4, 4, 4, 4, 2, 2, 1]
+
+
+def rank_program(g, core, T, topo):
+    me = T.rank_of(core)
+    if me is None:
+        return
+    A, F = AluOpType, ActivationFunctionType
+    V, S, P, Y = g.vector, g.scalar, g.tensor, g.sync
+    sem = T.sem
+    AND, SHR = A.bitwise_and, A.logical_shift_right
+
+    def bits(out, in_, shift, mask):
+        if shift and mask:
+            return V.tensor_scalar(out, in_, shift, mask, SHR, AND)
+        if shift:
+            return V.tensor_scalar(out, in_, shift, None, SHR)
+        return V.tensor_scalar(out, in_, mask, None, AND)
+
+    S.dma_start(T.land[:, 7, 16:32], T.place[:]).then_inc(sem.dl, 16)
+    Y.dma_start(T.land[:, 7, 0:16], T.when[:]).then_inc(sem.dl, 16)
+    Y.dma_start(T.trk[:], T.track[:]).then_inc(sem.dt, 16)
+    Y.dma_start(T.snd[:, 0:CUT], T.sound[:, 0:CUT]).then_inc(sem.dn0, 16)
+
+    V.memset(T.win[:, 0:ZS], 0.0).then_inc(sem.vy, 1)
+    V.memset(T.zb[:], 0.0).then_inc(sem.vz, 1)
+    V.memset(T.win[:, ZS:ZV], 0.0).then_inc(sem.vw, 1)
+    S.wait_ge(sem.vy, 1)
+    for k in range(ZV, L, ZS):
+        S.activation(T.win[:, k:k + ZS], T.win[:, 0:ZS], F.Copy).then_inc(sem.sz, 1)
+
+    g.iota(T.pi[:, 0:1], [[1, 1]], 0, 1).then_inc(sem.gi, 1)
+    g.wait_ge(sem.vz, 1)
+    others = [(me + d) % N for d in range(1, N)]
+    dst0 = T.cores[others[0]]
+    mask = topo.mask(core, dst0)
+    neng = len(topo.engines(core, dst0))
+    ids, dsts = [], []
+    for r in others:
+        rid, pid, _ = topo.addr(T.cores[r])
+        ids.append(DstId(rid=rid, pnc=pid))
+        dsts.append(T.land[:, (me - r - 1) % N, :])
+    for c in range(4):
+        if c == 2:
+            g.wait_ge(sem.dl, 32)
+            g.remote_dma_fused([RemoteDMATransfer(dst_ids=ids, dma_engine_mask=mask, remote_sem=sem.arr, srcs=[T.land[:, 7, :]], dsts=dsts)],
+                               local_sem=sem.ls)
+        g.affine_select(T.ec[:, c, :], T.zb[:, 0:8], [[-16, 8]], A.not_equal, 1.0 if c % 2 else 64.0, -c, 1).then_inc(sem.ge, 1)
+    for h in range(2):
+        g.affine_select(T.qb[:, h, :, :], T.zb[:, 0:64], [[-4, 2], [-16, 8], [-1, 4]], A.not_equal, -1.0, -8 * h, 1).then_inc(sem.gq, 1)
+    for h in range(2):
+        g.affine_select(T.rb[:, h, :], T.zb[:, 0:64], [[-2, 64]], A.not_equal, -1.0, -h, 1).then_inc(sem.gm, 1)
+    g.affine_select(T.i1[:], T.zb[:], [[-1, 128]], A.not_equal, 1.0, 0, 1).then_inc(sem.g1, 1)
+
+    V.wait_ge(sem.dt, 16)
+    Y.wait_ge(sem.vy, 1)
+    Y.wait_ge(sem.vw, 1)
+    Y.wait_ge(sem.sz, (L - ZV) // ZS)
+    for c, (sh, mk) in enumerate(((18, 0), (12, 63), (6, 63), (0, 63))):
+        for k in range(2):
+            hf = slice(256 * k, 256 * k + 256)
+            bits(T.dig[:, c, hf], T.trk[:, hf], sh, mk).then_inc(sem["vd%d" % c], 1)
+            S.wait_ge(sem["vd%d" % c], k + 1)
+            S.activation(T.dgb[:, c, hf], T.dig[:, c, hf], F.Copy, bias=0.0 if c % 2 else -32.0).then_inc(sem["sd%d" % c], 1)
+        Y.wait_ge(sem["sd%d" % c], 2)
+        Y.dma_start(T.win[c:128:16, :], T.dgb[:, c, :]).then_inc(sem.dw, 16)
+    Y.dma_start(T.snd[:, CUT:H + 16], T.sound[:, CUT:H + 16]).then_inc(sem.dn2, 16)
+    Y.dma_start(T.us[:, H:MID], T.sound[:, H:MID]).then_inc(sem.dn1, 16)
+    Y.dma_start(T.us[:, MID:L], T.sound[:, MID:L]).then_inc(sem.dn3, 16)
+    g.wait_ge(sem.dn1, 16)
+    g.dma_start(T.us[:, H:MID], T.sound[:, H + 1:MID + 1], accum_op=A.add, max_dma_last_dim=4096).then_inc(sem.ga0, 16)
+    g.wait_ge(sem.dn3, 16)
+    g.dma_start(T.us[:, MID:L - 1], T.sound[:, MID + 1:L], accum_op=A.add, max_dma_last_dim=4096).then_inc(sem.ga1, 16)
+
+    V.wait_ge(sem.gi, 1)
+    bits(T.mki[:, 0:1], T.pi[:, 0:1], 3, 1).then_inc(sem.vb, 1)
+    bits(T.mki[:, 1:2], T.pi[:, 0:1], 0, 1).then_inc(sem.vb, 1)
+    V.wait_ge(sem.ge, 4)
+    V.tensor_tensor(T.es[:, :, :], T.ec[:, 0:4:2, :], T.ec[:, 1:4:2, :], A.add).then_inc(sem.ve, 1)
+    V.wait_ge(sem.gq, 2)
+    V.tensor_tensor(T.qn[:, 0, :, 0, :], T.qb[:, 0, :, :], T.qb[:, 1, :, :], A.add).then_inc(sem.vn, 1)
+    V.tensor_tensor(T.qn[:, 0, :, 1, :], T.qb[:, 0, :, :], T.qb[:, 1, :, :], A.add).then_inc(sem.vk, 1)
+    V.tensor_tensor(T.qn[:, 1, :, 0, :], T.qb[:, 0, :, :], T.qb[:, 1, :, :], A.add).then_inc(sem.vk, 1)
+    V.wait_ge(sem.gm, 2)
+    V.tensor_tensor(T.rm[:], T.rb[:, 0, :], T.rb[:, 1, :], A.add).then_inc(sem.vk, 1)
+    V.wait_ge(sem.vb, 2)
+    V.tensor_scalar(T.mkf[:, 0:1], T.mki[:, 0:1], -1.0, 1.0, A.mult, A.add).then_inc(sem.vm, 1)
+    V.tensor_copy(T.mkf[:, 1:2], T.mki[:, 0:1]).then_inc(sem.vm, 1)
+    V.tensor_scalar(T.mkf[:, 2:3], T.mki[:, 1:2], -0.5, 0.5, A.mult, A.add).then_inc(sem.vm, 1)
+    V.tensor_scalar(T.mkf[:, 3:4], T.mki[:, 1:2], 0.5, None, A.mult).then_inc(sem.vm, 1)
+    V.wait_ge(sem.ve, 1)
+    V.tensor_tensor(T.r16[:, 0:8], T.es[:, 0, :], T.es[:, 1, :], A.add).then_inc(sem.vk, 1)
+    V.tensor_tensor(T.r16[:, 8:16], T.es[:, 0, :], T.es[:, 1, :], A.subtract).then_inc(sem.vk, 1)
+    V.wait_ge(sem.vn, 1)
+    V.tensor_scalar(T.qn[:, 1, :, 1, :], T.qn[:, 0, :, 0, :], -1.0, None, A.mult).then_inc(sem.vk, 1)
+    V.wait_ge(sem.g1, 1)
+    V.tensor_copy(T.i32[:], T.i1[:]).then_inc(sem.vk, 1)
+
+    def vg(x, i, c0, c1):
+        V.wait_ge(sem["cp%d" % x], i + 1)
+        V.tensor_copy(T["v%d" % x][:, 16 * c0:16 * c1], T.win[:, 0:L].indirect(T["l%d" % x][:, c0:c1])).then_inc(sem["gv%d" % x], 1)
+
+    def sg(x, i):
+        S.wait_ge(sem["cp%d" % x], i + 1)
+        S.activation(T["v%d" % x][:, 16 * VW:1024], T.win[:, 0:L].indirect(T["l%d" % x][:, VW:64]), F.Copy).then_inc(sem["gs%d" % x], 1)
+
+    def prep(x):
+        sl = slice(4 * x, 4 * x + 4)
+        vp = sem["vp%d" % x]
+        bits(T.pxy[:, 0, sl, :], T.land[:, sl, 16:32], 12, 0).then_inc(vp, 1)
+        bits(T.pxy[:, 1, sl, :], T.land[:, sl, 16:32], 0, 4095).then_inc(vp, 1)
+        V.tensor_copy(T.tf[:, sl, :], T.land[:, sl, 0:16]).then_inc(vp, 1)
+        V.wait_ge(vp, 3)
+        for c in range(2):
+            for h in range(2):
+                V.tensor_scalar(T.cx[:, c, sl, h:32:2], T.pxy[:, c, sl, :], -2048.0, T.mkf[:, h:h + 1], A.add, A.mult).then_inc(vp, 1)
+
+    def times(x, i):
+        P.wait_ge(sem["cp%d" % x], i + 1)
+        P.matmul(T["q%d" % x][:, 0:64], T.i32[:], T.tf[:, 4 * x:4 * x + 4, :], True, False).then_inc(sem["tr%d" % x], 1)
+
+    def places(x, i):
+        if i:
+            P.wait_ge(sem["ab%d" % x], NA * i)
+        for f in range(2):
+            for c in range(2):
+                P.matmul(T["p%d%d" % (x, f)][:, 0:16, :], T.cx[:, c, 4 * x:4 * x + 4, :], T.qn[:, c, f, :, :], c == 0, False).then_inc(sem["st%d" % x], 1)
+
+    def rows(x, i):
+        P.wait_ge(sem["gv%d" % x], (2 - x) * (i + 1))
+        P.wait_ge(sem["gs%d" % x], i + 1)
+        for b in range(8):
+            P.matmul(T["p%d%d" % (x, b // 4)][:, 0:16, b % 4], T["v%d" % x][:, b:1024:8], T.r16[:], False, b % 4 == 3).then_inc(sem["st%d" % x], 1)
+
+    def absolute(x, i):
+        for f in range(2):
+            S.wait_ge(sem["st%d" % x], 12 * i + 8 + 4 * f)
+            for c in ((slice(0, 16),), (slice(0, 8), slice(8, 16)))[f]:
+                for h in range(2):
+                    S.activation(T["a%d" % x][:, c, 8 * h + 4 * f:8 * h + 4 * f + 4], T["p%d%d" % (x, f)][:, c, :], F.Abs,
+                                 scale=T.mkf[:, 2 + h:3 + h]).then_inc(sem["ab%d" % x], 1)
+
+    def back(x, i):
+        for c in range(2):
+            P.wait_ge(sem["ab%d" % x], NA * i + 4 + 2 * c)
+            P.matmul(T["q%d" % x][:, 0:64], T["a%d" % x][:, 8 * c:8 * c + 8, :], T.rm[:], False, c == 1).then_inc(sem["tr%d" % x], 1)
+
+    def newlist(x, i):
+        V.wait_ge(sem["tr%d" % x], 3 * (i + 1))
+        V.tensor_copy(T["l%d" % x][:], T["q%d" % x][:, 0:64]).then_inc(sem["cp%d" % x], 1)
+
+    npiece, nout = [0], [0]
+
+    def pieces(n):
+        for _ in range(n):
+            k = npiece[0]
+            if k == 0:
+                P.wait_ge(sem.dn0, 16)
+            if 512 * k + 513 > CUT >= 512 * k + 1:
+                P.wait_ge(sem.dn2, 16)
+            if k >= 2:
+                P.wait_ge(sem.vu, k - 1)
+            w = T["w%d" % (k % 2)]
+            P.matmul(w[:], T.i1[:], T.snd[:, 512 * k:512 * k + 512], True, False).then_inc(sem.pu, 1)
+            P.matmul(w[:], T.i1[:], T.snd[:, 512 * k + 1:512 * k + 513], False, True).then_inc(sem.pu, 1)
+            npiece[0] += 1
+
+    def out(n):
+        for _ in range(n):
+            k = nout[0]
+            V.wait_ge(sem.pu, 2 * k + 2)
+            V.tensor_copy(T.us[:, 512 * k:512 * k + 512], T["w%d" % (k % 2)][:]).then_inc(sem.vu, 1)
+            nout[0] += 1
+
+    P.wait_ge(sem.g1, 1)
+    pieces(UP[0])
+    out(UP[0])
+    V.wait_ge(sem.dl, 32)
+    V.wait_ge(sem.arr, 7 * neng)
+    for x in range(2):
+        V.tensor_copy(T["l%d" % x][:], T.land[:, 4 * x:4 * x + 4, 0:16]).then_inc(sem["cp%d" % x], 1)
+    V.wait_ge(sem.vm, 4)
+    prep(0)
+    prep(1)
+    V.wait_ge(sem.dw, 64)
+    S.wait_ge(sem.vm, 4)
+    S.wait_ge(sem.dw, 64)
+    pieces(UP[1])
+    P.wait_ge(sem.vk, 7)
+
+    for i in range(R):
+        vg(0, i, 0, VM)
+        if i:
+            newlist(1, i - 1)
+        vg(0, i, VM, VW)
+        vg(1, i, 0, VW)
+        out(UP[i + 1])
+        newlist(0, i)
+        sg(0, i)
+        sg(1, i)
+        absolute(0, i)
+        absolute(1, i)
+        if i == 0:
+            for x in range(2):
+                P.wait_ge(sem["vp%d" % x], 7)
+                places(x, 0)
+                times(x, 0)
+            rows(0, 0)
+        else:
+            rows(0, i)
+            times(1, i)
+        rows(1, i)
+        back(0, i)
+        back(1, i)
+        if i < R - 1:
+            places(0, i + 1)
+            places(1, i + 1)
+            pieces(UP[i + 2])
+            times(0, i + 1)
+
+    def final(x, q, c0, c1):
+        o, src = T["u%d" % x][:, 16 * c0:16 * c1], T.us[:, 0:L].indirect(T["l%d" % x][:, c0:c1])
+        if q is V:
+            V.tensor_copy(o, src).then_inc(sem["fv%d" % x], 1)
+        else:
+            S.activation(o, src, F.Copy).then_inc(sem["fs%d" % x], 1)
+
+    for q in (S, V):
+        q.wait_ge(sem.ga0, 16)
+        q.wait_ge(sem.ga1, 16)
+        q.wait_ge(sem.vu, sum(UP))
+        q.wait_ge(sem.cp0, R + 1)
+    final(0, V, 0, VF)
+    final(0, S, VF, 64)
+    newlist(1, R - 1)
+    V.wait_ge(sem.cp1, R + 1)
+    S.wait_ge(sem.cp1, R + 1)
+    final(1, V, 0, 16)
+    final(1, S, 16, 32)
+    final(1, V, 32, 40)
+    final(1, S, 40, 48)
+    final(1, V, 48, 56)
+    final(1, S, 56, 64)
+
+    nloc = 0
+    for j, slots in enumerate(CALLS):
+        x = slots[0] // 4
+        g.wait_ge(sem["fv%d" % x], max(j, 1))
+        g.wait_ge(sem["fs%d" % x], max(j, 1))
+        tr = []
+        for k, s in enumerate(slots):
+            d = T.cores[(me + 1 + s) % N]
+            rid, pid, _ = topo.addr(d)
+            e = topo.engines(core, d)
+            w = len(e) // WIDTH[s]
+            tr.append(RemoteDMATransfer(dst_ids=[DstId(rid=rid, pnc=pid)], dma_engine_mask=sum(1 << m for m in e[w * k:w * k + w]),
+                                        remote_sem=sem["uq%d" % me], srcs=[T["u%d" % x][:, 256 * (s % 4):256 * (s % 4) + 256]],
+                                        dsts=[T.ul[:, me, :]]))
+            nloc += w
+        g.remote_dma_fused(tr, local_sem=sem.lu)
+
+    P.wait_ge(sem.vu, sum(UP))
+    for q in range(N):
+        if q == me:
+            P.wait_ge(sem.fv1, 3)
+            P.wait_ge(sem.fs1, 3)
+        else:
+            P.wait_ge(sem["uq%d" % q], len(topo.engines(T.cores[q], core)) // WIDTH[(me - q - 1) % N])
+        for h in range(2):
+            src = T.u1[:, 768 + 128 * h:896 + 128 * h] if q == me else T.ul[:, q, 128 * h:128 * h + 128]
+            P.matmul(T["w%d" % h][:, 0:128], T.i1[:], src, q == 0, q == N - 1).then_inc(sem["yp%d" % h], 1)
+    V.wait_ge(sem.yp0, N)
+    V.tensor_copy(T.ysb[:, 0:128], T.w0[:, 0:128]).then_inc(sem.yc0, 1)
+    Y.wait_ge(sem.yc0, 1)
+    Y.dma_start(T.y[:, 0:128], T.ysb[:, 0:128]).then_inc(sem.dy0, 16)
+    Y.wait_ge(sem.dy0, 16)
+    S.wait_ge(sem.yp1, N)
+    S.activation(T.ysb[:, 128:256], T.w1[:, 0:128], F.Copy).then_inc(sem.yc1, 1)
+    S.wait_ge(sem.yc1, 1)
+    S.dma_start(T.y[:, 128:256], T.ysb[:, 128:256]).then_inc(sem.dy1, 16)
+    S.wait_ge(sem.dy1, 16)
+    g.wait_ge(sem.ls, neng)
+    g.wait_ge(sem.lu, nloc)

@@ -1,68 +1,65 @@
 from concourse.bass import DstId, RemoteDMATransfer
-from concourse.mybir import AluOpType, ActivationFunctionType
+from concourse.mybir import AluOpType, ActivationFunctionType, AxisListType
 
 N = 8
 R = 5
 L = 8192
-ZV, ZS = 5632, 512
-VW = 32
-VM = 20
-VF = 32
-UP = [0, 1, 1, 1, 1, 0, 0]
-H = 512 * sum(UP)
-CUT = 1024
+REG = 4096
+ZA = 2304
+ZV = 5632
+ZG, Z0, ZS = 7680, 384, 1024
+NB = 4
+VW = (14, 14, 14, 14)
+VW0 = (18, 20, 12, 14)
+VF = (12, 14, 12, 10)
+LAGR = 2
+LAGN = 3
+VO = 0
+LAGB = 1
+LEAD = 1
+PO = 2
+PW = 256
+NW = 4
+PRE_S, PRE_V = 2, 0
+IN_S = [0, 1, 1, 0, 1, 0, 1, 0, 1, 0, 0, 0, 1, 0, 0, 0, 1, 0, 0, 0]
+IN_V = [0, 0, 0, 0, 0, 0, 0, 0, 0, 0, 0, 0, 0, 0, 0, 0, 0, 0, 0, 0]
+NP = PRE_S + PRE_V + sum(IN_S) + sum(IN_V)
+H = PW * NP
+CUTS = [0, 1040, 1040, H + 16]
 MID = 5632
-NA = 6
 SCRATCH = {
     "land": ("sbuf", [128, 8, 32], "int32"),
     "pxy": ("sbuf", [128, 2, 8, 16], "int32"),
-    "cx": ("sbuf", [128, 2, 8, 32], "float16"),
-    "tf": ("sbuf", [128, 8, 16], "float32"),
-    "win": ("sbuf", [128, L], "bfloat16"),
-    "snd": ("sbuf", [128, 4608], "bfloat16"),
+    "cx": ("sbuf", [128, 2, 8, 64], "float16"),
+    "win": ("sbuf", [128, L], "int32"),
+    "snd": ("sbuf", [128, H + 16], "bfloat16"),
     "us": ("sbuf", [128, L], "bfloat16"),
     "trk": ("sbuf", [128, 512], "int32"),
-    "dig": ("sbuf", [128, 4, 512], "int32"),
-    "dgb": ("sbuf", [128, 4, 512], "bfloat16"),
-    "v0": ("sbuf", [128, 1024], "bfloat16"),
-    "v1": ("sbuf", [128, 1024], "bfloat16"),
-    "u0": ("sbuf", [128, 1024], "bfloat16"),
-    "u1": ("sbuf", [128, 1024], "bfloat16"),
-    "a0": ("sbuf", [128, 16, 16], "float32"),
-    "a1": ("sbuf", [128, 16, 16], "float32"),
-    "l0": ("sbuf", [128, 64], "uint16"),
-    "l1": ("sbuf", [128, 64], "uint16"),
+    "dig": ("sbuf", [128, 2, 512], "int32"),
+    "uo": ("sbuf", [128, 2048], "bfloat16"),
     "ul": ("sbuf", [128, 8, 256], "bfloat16"),
     "ysb": ("sbuf", [128, 256], "float32"),
-    "zb": ("sbuf", [128, 128], "bfloat16"),
+    "zb": ("sbuf", [128, 192], "bfloat16"),
     "i1": ("sbuf", [128, 128], "bfloat16"),
-    "i32": ("sbuf", [128, 128], "float32"),
-    "ec": ("sbuf", [128, 4, 8], "bfloat16"),
-    "es": ("sbuf", [128, 2, 8], "bfloat16"),
-    "r16": ("sbuf", [128, 16], "bfloat16"),
-    "qb": ("sbuf", [128, 2, 2, 32], "bfloat16"),
-    "qn": ("sbuf", [128, 2, 2, 2, 32], "float16"),
-    "rb": ("sbuf", [128, 2, 64], "bfloat16"),
-    "rm": ("sbuf", [128, 64], "float32"),
-    "pi": ("sbuf", [128, 8], "int32"),
-    "mki": ("sbuf", [128, 8], "int32"),
+    "r32": ("sbuf", [128, 8, 4], "bfloat16"),
+    "qz": ("sbuf", [128, 32, 6], "bfloat16"),
+    "rb": ("sbuf", [128, 4, 32], "bfloat16"),
+    "pi": ("sbuf", [128, 4], "int32"),
+    "mki": ("sbuf", [128, 4], "int32"),
     "mkf": ("sbuf", [128, 8], "float32"),
-    "p00": ("psum", [128, 128, 4], "float32"),
-    "p01": ("psum", [128, 128, 4], "float32"),
-    "p10": ("psum", [128, 128, 4], "float32"),
-    "p11": ("psum", [128, 128, 4], "float32"),
-    "q0": ("psum", [128, 512], "float32"),
-    "q1": ("psum", [128, 512], "float32"),
-    "w0": ("psum", [128, 512], "float32"),
-    "w1": ("psum", [128, 512], "float32"),
+    "lst": ("sbuf", [128, 128], "uint16"),
+    "a": ("sbuf", [128, 36 * NB, 4], "float16"),
 }
-SEMAPHORES = (["vz", "vy", "gi", "ge", "gq", "gm", "g1", "vb", "vm", "dl", "dt", "vp0", "vp1", "vk", "ve", "vn", "vw", "sz", "dw",
-               "arr", "ls", "lu", "yp0", "yp1", "yc0", "yc1", "dy0", "dy1", "dn0", "dn1", "dn2", "dn3", "ga0", "ga1", "pu", "vu"]
-              + ["vd%d" % c for c in range(4)] + ["sd%d" % c for c in range(4)]
-              + ["%s%d" % (k, x) for k in ("gv", "gs", "st", "ab", "tr", "cp", "fv", "fs") for x in range(2)]
+for _x in range(NB):
+    SCRATCH["v%d" % _x] = ("sbuf", [128, 512], "float16")
+    SCRATCH["p%d" % _x] = ("psum", [128, 32, 4, 4], "float32")
+for _x in range(NW):
+    SCRATCH["w%d" % _x] = ("psum", [128, 512], "float32")
+SEMAPHORES = (["vz", "vy", "gi", "gz", "ge", "gq", "gm", "g1", "vb", "vm", "dl", "dt", "vp", "vx", "sx", "sn", "sz", "dw", "vd0", "vd1",
+               "arr", "ls", "lu", "yp0", "yp1", "yc0", "yc1", "dy0", "dy1", "ds0", "ds1", "ds2", "dn1", "dn3", "ga0", "ga1",
+               "pu", "ov", "ow", "vw", "sy", "fo", "l0", "za"]
+              + ["%s%d" % (k, x) for k in ("gv", "gs", "st", "ab", "tr", "cp", "fu") for x in range(NB)]
               + ["uq%d" % q for q in range(N)])
-CALLS = [(0, 1, 2, 3), (4, 5), (6,)]
-WIDTH = [4, 4, 4, 4, 2, 2, 1]
 
 
 def rank_program(g, core, T, topo):
@@ -81,20 +78,38 @@ def rank_program(g, core, T, topo):
             return V.tensor_scalar(out, in_, shift, None, SHR)
         return V.tensor_scalar(out, in_, mask, None, AND)
 
+    def sound(k):
+        if CUTS[k] < CUTS[k + 1]:
+            Y.dma_start(T.snd[:, CUTS[k]:CUTS[k + 1]], T.sound[:, CUTS[k]:CUTS[k + 1]]).then_inc(sem["ds%d" % k], 16)
+
     S.dma_start(T.land[:, 7, 16:32], T.place[:]).then_inc(sem.dl, 16)
     Y.dma_start(T.land[:, 7, 0:16], T.when[:]).then_inc(sem.dl, 16)
-    Y.dma_start(T.trk[:], T.track[:]).then_inc(sem.dt, 16)
-    Y.dma_start(T.snd[:, 0:CUT], T.sound[:, 0:CUT]).then_inc(sem.dn0, 16)
+    Y.dma_start(T.trk[:, 0:REG // 16], T.track[:, 0:REG]).then_inc(sem.dt, 16)
+    S.dma_start(T.trk[:, REG // 16:512], T.track[:, REG:L]).then_inc(sem.dt, 16)
+    sound(0)
+    sound(1)
 
-    V.memset(T.win[:, 0:ZS], 0.0).then_inc(sem.vy, 1)
+    V.memset(T.win[:, 0:Z0], 0).then_inc(sem.vy, 1)
     V.memset(T.zb[:], 0.0).then_inc(sem.vz, 1)
-    V.memset(T.win[:, ZS:ZV], 0.0).then_inc(sem.vw, 1)
+    V.memset(T.win[:, Z0:ZS], 0).then_inc(sem.vy, 1)
+    V.memset(T.win[:, ZS:ZA], 0).then_inc(sem.vy, 1)
     S.wait_ge(sem.vy, 1)
-    for k in range(ZV, L, ZS):
-        S.activation(T.win[:, k:k + ZS], T.win[:, 0:ZS], F.Copy).then_inc(sem.sz, 1)
+    S.activation(T.win[:, ZA:ZA + Z0], T.win[:, 0:Z0], F.Copy).then_inc(sem.sz, 1)
+    S.wait_ge(sem.vy, 2)
+    nz = [1, 1]
+    for k in range(ZA + Z0, REG, ZS):
+        w = min(ZS, REG - k)
+        S.activation(T.win[:, k:k + w], T.win[:, 0:w], F.Copy).then_inc(sem.sz, 1)
+        nz[0] += 1
+    z1 = 2 * ZG - L
+    S.wait_ge(sem.gz, 1)
+    S.activation(T.win[:, z1:ZG], T.win[:, ZG:L], F.Copy).then_inc(sem.sy, 1)
+    for k in range(ZV, z1, L - ZG):
+        w = min(L - ZG, z1 - k)
+        S.activation(T.win[:, k:k + w], T.win[:, ZG:ZG + w], F.Copy).then_inc(sem.sy, 1)
+        nz[1] += 1
 
-    g.iota(T.pi[:, 0:1], [[1, 1]], 0, 1).then_inc(sem.gi, 1)
-    g.wait_ge(sem.vz, 1)
+    g.iota(T.win[:, ZG:L], [[0, L - ZG]], 0, 0).then_inc(sem.gz, 1)
     others = [(me + d) % N for d in range(1, N)]
     dst0 = T.cores[others[0]]
     mask = topo.mask(core, dst0)
@@ -104,31 +119,37 @@ def rank_program(g, core, T, topo):
         rid, pid, _ = topo.addr(T.cores[r])
         ids.append(DstId(rid=rid, pnc=pid))
         dsts.append(T.land[:, (me - r - 1) % N, :])
-    for c in range(4):
-        if c == 2:
-            g.wait_ge(sem.dl, 32)
-            g.remote_dma_fused([RemoteDMATransfer(dst_ids=ids, dma_engine_mask=mask, remote_sem=sem.arr, srcs=[T.land[:, 7, :]], dsts=dsts)],
-                               local_sem=sem.ls)
-        g.affine_select(T.ec[:, c, :], T.zb[:, 0:8], [[-16, 8]], A.not_equal, 1.0 if c % 2 else 64.0, -c, 1).then_inc(sem.ge, 1)
-    for h in range(2):
-        g.affine_select(T.qb[:, h, :, :], T.zb[:, 0:64], [[-4, 2], [-16, 8], [-1, 4]], A.not_equal, -1.0, -8 * h, 1).then_inc(sem.gq, 1)
-    for h in range(2):
-        g.affine_select(T.rb[:, h, :], T.zb[:, 0:64], [[-2, 64]], A.not_equal, -1.0, -h, 1).then_inc(sem.gm, 1)
-    g.affine_select(T.i1[:], T.zb[:], [[-1, 128]], A.not_equal, 1.0, 0, 1).then_inc(sem.g1, 1)
+    g.wait_ge(sem.dl, 32)
+    g.remote_dma_fused([RemoteDMATransfer(dst_ids=ids, dma_engine_mask=mask, remote_sem=sem.arr, srcs=[T.land[:, 7, :]], dsts=dsts)],
+                       local_sem=sem.ls)
+    g.wait_ge(sem.vz, 1)
+    g.affine_select(T.i1[:], T.zb[:, 0:128], [[-1, 128]], A.not_equal, 1.0, 0, 1).then_inc(sem.g1, 1)
+    g.iota(T.pi[:], [[-4, 4]], 16, 1).then_inc(sem.gi, 1)
+    g.affine_select(T.qz[:], T.zb[:], [[-16, 8], [-1, 4], [128, 6]], A.not_equal, 1.0, -384, 1).then_inc(sem.gq, 1)
+    g.affine_select(T.r32[:], T.zb[:, 0:32], [[-16, 8], [0, 4]], A.not_equal, 1.0, -2, 1).then_inc(sem.ge, 1)
+    for h in range(1, 4):
+        g.wait_ge(sem.gq, h)
+        g.affine_select(T.qz[:, :, 3], T.qz[:, :, 3], [[-16, 8], [-1, 4]], A.not_equal, 1.0, -4 * h, 1).then_inc(sem.gq, 1)
+        if h < 3:
+            g.wait_ge(sem.ge, 1)
+            g.affine_select(T.r32[:, :, h - 1:4:2], T.r32[:, :, h - 1:4:2], [[-16, 8], [-1, 2]], A.not_equal, 3.0 - 2 * h, 0, 1).then_inc(sem.ge, 1)
+    g.affine_select(T.rb[:], T.zb[:, 0:128], [[-1, 4], [-4, 32]], A.not_equal, -1.0, 0, 1).then_inc(sem.gm, 1)
 
-    V.wait_ge(sem.dt, 16)
-    Y.wait_ge(sem.vy, 1)
+    V.wait_ge(sem.dt, 32)
+    bits(T.dig[:, 0, :], T.trk[:], 12, 0).then_inc(sem.vd0, 1)
+    bits(T.dig[:, 1, :], T.trk[:], 0, 4095).then_inc(sem.vd1, 1)
+    V.memset(T.win[:, REG:ZV], 0).then_inc(sem.vw, 1)
+    Y.wait_ge(sem.vy, 3)
+    Y.wait_ge(sem.sz, nz[0])
+    for c in range(2):
+        Y.wait_ge(sem["vd%d" % c], 1)
+        Y.dma_start(T.win[c:128:16, 0:REG], T.dig[:, c, 0:REG // 16]).then_inc(sem.dw, 16)
     Y.wait_ge(sem.vw, 1)
-    Y.wait_ge(sem.sz, (L - ZV) // ZS)
-    for c, (sh, mk) in enumerate(((18, 0), (12, 63), (6, 63), (0, 63))):
-        for k in range(2):
-            hf = slice(256 * k, 256 * k + 256)
-            bits(T.dig[:, c, hf], T.trk[:, hf], sh, mk).then_inc(sem["vd%d" % c], 1)
-            S.wait_ge(sem["vd%d" % c], k + 1)
-            S.activation(T.dgb[:, c, hf], T.dig[:, c, hf], F.Copy, bias=0.0 if c % 2 else -32.0).then_inc(sem["sd%d" % c], 1)
-        Y.wait_ge(sem["sd%d" % c], 2)
-        Y.dma_start(T.win[c:128:16, :], T.dgb[:, c, :]).then_inc(sem.dw, 16)
-    Y.dma_start(T.snd[:, CUT:H + 16], T.sound[:, CUT:H + 16]).then_inc(sem.dn2, 16)
+    Y.wait_ge(sem.sy, nz[1])
+    Y.wait_ge(sem.gz, 1)
+    for c in range(2):
+        Y.dma_start(T.win[c:128:16, REG:L], T.dig[:, c, REG // 16:512]).then_inc(sem.dw, 16)
+    sound(2)
     Y.dma_start(T.us[:, H:MID], T.sound[:, H:MID]).then_inc(sem.dn1, 16)
     Y.dma_start(T.us[:, MID:L], T.sound[:, MID:L]).then_inc(sem.dn3, 16)
     g.wait_ge(sem.dn1, 16)
@@ -136,202 +157,186 @@ def rank_program(g, core, T, topo):
     g.wait_ge(sem.dn3, 16)
     g.dma_start(T.us[:, MID:L - 1], T.sound[:, MID + 1:L], accum_op=A.add, max_dma_last_dim=4096).then_inc(sem.ga1, 16)
 
+    made, outs, loaded = [0], [], [0]
+
+    def piece(early=False):
+        k = made[0]
+        if k >= NP or k - NW >= len(outs) or (early and PW * k + PW + 1 > CUTS[2]):
+            return
+        if k == 0:
+            P.wait_ge(sem.g1, 1)
+        while CUTS[loaded[0]] < PW * k + PW + 1:
+            if CUTS[loaded[0]] < CUTS[loaded[0] + 1]:
+                P.wait_ge(sem["ds%d" % loaded[0]], 16)
+            loaded[0] += 1
+        if k >= NW:
+            P.wait_ge(*outs[k - NW])
+        w = T["w%d" % (k % NW)][:, 0:PW]
+        P.matmul(w, T.i1[:], T.snd[:, PW * k:PW * k + PW], True, False).then_inc(sem.pu, 1)
+        P.matmul(w, T.i1[:], T.snd[:, PW * k + 1:PW * k + PW + 1], False, True).then_inc(sem.pu, 1)
+        made[0] += 1
+
+    nout = {"ov": 0, "ow": 0}
+
+    def out(q, n):
+        for _ in range(n):
+            k = len(outs)
+            q.wait_ge(sem.pu, 2 * k + 2)
+            o, w = T.us[:, PW * k:PW * k + PW], T["w%d" % (k % NW)][:, 0:PW]
+            s = "ov" if q is V else "ow"
+            (V.tensor_copy(o, w) if q is V else S.activation(o, w, F.Copy)).then_inc(sem[s], 1)
+            nout[s] += 1
+            outs.append((sem[s], nout[s]))
+
+    for _ in range(NW):
+        piece(True)
+
     V.wait_ge(sem.gi, 1)
-    bits(T.mki[:, 0:1], T.pi[:, 0:1], 3, 1).then_inc(sem.vb, 1)
-    bits(T.mki[:, 1:2], T.pi[:, 0:1], 0, 1).then_inc(sem.vb, 1)
-    V.wait_ge(sem.ge, 4)
-    V.tensor_tensor(T.es[:, :, :], T.ec[:, 0:4:2, :], T.ec[:, 1:4:2, :], A.add).then_inc(sem.ve, 1)
-    V.wait_ge(sem.gq, 2)
-    V.tensor_tensor(T.qn[:, 0, :, 0, :], T.qb[:, 0, :, :], T.qb[:, 1, :, :], A.add).then_inc(sem.vn, 1)
-    V.tensor_tensor(T.qn[:, 0, :, 1, :], T.qb[:, 0, :, :], T.qb[:, 1, :, :], A.add).then_inc(sem.vk, 1)
-    V.tensor_tensor(T.qn[:, 1, :, 0, :], T.qb[:, 0, :, :], T.qb[:, 1, :, :], A.add).then_inc(sem.vk, 1)
-    V.wait_ge(sem.gm, 2)
-    V.tensor_tensor(T.rm[:], T.rb[:, 0, :], T.rb[:, 1, :], A.add).then_inc(sem.vk, 1)
-    V.wait_ge(sem.vb, 2)
-    V.tensor_scalar(T.mkf[:, 0:1], T.mki[:, 0:1], -1.0, 1.0, A.mult, A.add).then_inc(sem.vm, 1)
-    V.tensor_copy(T.mkf[:, 1:2], T.mki[:, 0:1]).then_inc(sem.vm, 1)
-    V.tensor_scalar(T.mkf[:, 2:3], T.mki[:, 1:2], -0.5, 0.5, A.mult, A.add).then_inc(sem.vm, 1)
-    V.tensor_scalar(T.mkf[:, 3:4], T.mki[:, 1:2], 0.5, None, A.mult).then_inc(sem.vm, 1)
-    V.wait_ge(sem.ve, 1)
-    V.tensor_tensor(T.r16[:, 0:8], T.es[:, 0, :], T.es[:, 1, :], A.add).then_inc(sem.vk, 1)
-    V.tensor_tensor(T.r16[:, 8:16], T.es[:, 0, :], T.es[:, 1, :], A.subtract).then_inc(sem.vk, 1)
-    V.wait_ge(sem.vn, 1)
-    V.tensor_scalar(T.qn[:, 1, :, 1, :], T.qn[:, 0, :, 0, :], -1.0, None, A.mult).then_inc(sem.vk, 1)
-    V.wait_ge(sem.g1, 1)
-    V.tensor_copy(T.i32[:], T.i1[:]).then_inc(sem.vk, 1)
-
-    def vg(x, i, c0, c1):
-        V.wait_ge(sem["cp%d" % x], i + 1)
-        V.tensor_copy(T["v%d" % x][:, 16 * c0:16 * c1], T.win[:, 0:L].indirect(T["l%d" % x][:, c0:c1])).then_inc(sem["gv%d" % x], 1)
-
-    def sg(x, i):
-        S.wait_ge(sem["cp%d" % x], i + 1)
-        S.activation(T["v%d" % x][:, 16 * VW:1024], T.win[:, 0:L].indirect(T["l%d" % x][:, VW:64]), F.Copy).then_inc(sem["gs%d" % x], 1)
-
-    def prep(x):
-        sl = slice(4 * x, 4 * x + 4)
-        vp = sem["vp%d" % x]
-        bits(T.pxy[:, 0, sl, :], T.land[:, sl, 16:32], 12, 0).then_inc(vp, 1)
-        bits(T.pxy[:, 1, sl, :], T.land[:, sl, 16:32], 0, 4095).then_inc(vp, 1)
-        V.tensor_copy(T.tf[:, sl, :], T.land[:, sl, 0:16]).then_inc(vp, 1)
-        V.wait_ge(vp, 3)
-        for c in range(2):
-            for h in range(2):
-                V.tensor_scalar(T.cx[:, c, sl, h:32:2], T.pxy[:, c, sl, :], -2048.0, T.mkf[:, h:h + 1], A.add, A.mult).then_inc(vp, 1)
-
-    def times(x, i):
-        P.wait_ge(sem["cp%d" % x], i + 1)
-        P.matmul(T["q%d" % x][:, 0:64], T.i32[:], T.tf[:, 4 * x:4 * x + 4, :], True, False).then_inc(sem["tr%d" % x], 1)
-
-    def places(x, i):
-        if i:
-            P.wait_ge(sem["ab%d" % x], NA * i)
-        for f in range(2):
-            for c in range(2):
-                P.matmul(T["p%d%d" % (x, f)][:, 0:16, :], T.cx[:, c, 4 * x:4 * x + 4, :], T.qn[:, c, f, :, :], c == 0, False).then_inc(sem["st%d" % x], 1)
-
-    def rows(x, i):
-        P.wait_ge(sem["gv%d" % x], (2 - x) * (i + 1))
-        P.wait_ge(sem["gs%d" % x], i + 1)
-        for b in range(8):
-            P.matmul(T["p%d%d" % (x, b // 4)][:, 0:16, b % 4], T["v%d" % x][:, b:1024:8], T.r16[:], False, b % 4 == 3).then_inc(sem["st%d" % x], 1)
-
-    def absolute(x, i):
-        for f in range(2):
-            S.wait_ge(sem["st%d" % x], 12 * i + 8 + 4 * f)
-            for c in ((slice(0, 16),), (slice(0, 8), slice(8, 16)))[f]:
-                for h in range(2):
-                    S.activation(T["a%d" % x][:, c, 8 * h + 4 * f:8 * h + 4 * f + 4], T["p%d%d" % (x, f)][:, c, :], F.Abs,
-                                 scale=T.mkf[:, 2 + h:3 + h]).then_inc(sem["ab%d" % x], 1)
-
-    def back(x, i):
-        for c in range(2):
-            P.wait_ge(sem["ab%d" % x], NA * i + 4 + 2 * c)
-            P.matmul(T["q%d" % x][:, 0:64], T["a%d" % x][:, 8 * c:8 * c + 8, :], T.rm[:], False, c == 1).then_inc(sem["tr%d" % x], 1)
-
-    def newlist(x, i):
-        V.wait_ge(sem["tr%d" % x], 3 * (i + 1))
-        V.tensor_copy(T["l%d" % x][:], T["q%d" % x][:, 0:64]).then_inc(sem["cp%d" % x], 1)
-
-    npiece, nout = [0], [0]
-
-    def pieces(n):
-        for _ in range(n):
-            k = npiece[0]
-            if k == 0:
-                P.wait_ge(sem.dn0, 16)
-            if 512 * k + 513 > CUT >= 512 * k + 1:
-                P.wait_ge(sem.dn2, 16)
-            if k >= 2:
-                P.wait_ge(sem.vu, k - 1)
-            w = T["w%d" % (k % 2)]
-            P.matmul(w[:], T.i1[:], T.snd[:, 512 * k:512 * k + 512], True, False).then_inc(sem.pu, 1)
-            P.matmul(w[:], T.i1[:], T.snd[:, 512 * k + 1:512 * k + 513], False, True).then_inc(sem.pu, 1)
-            npiece[0] += 1
-
-    def out(n):
-        for _ in range(n):
-            k = nout[0]
-            V.wait_ge(sem.pu, 2 * k + 2)
-            V.tensor_copy(T.us[:, 512 * k:512 * k + 512], T["w%d" % (k % 2)][:]).then_inc(sem.vu, 1)
-            nout[0] += 1
-
-    P.wait_ge(sem.g1, 1)
-    pieces(UP[0])
-    out(UP[0])
+    bits(T.mki[:], T.pi[:], 2, 3).then_inc(sem.vb, 1)
+    for k in range(3):
+        V.memset(T.a[:, k:36 * NB:4, :], 0.0 if k else 2048.0).then_inc(sem.za, 1)
+    out(V, PRE_V)
+    V.wait_ge(sem.vb, 1)
+    V.tensor_scalar(T.mkf[:, 0:4], T.mki[:], 0.0, None, A.is_equal).then_inc(sem.vm, 1)
+    V.tensor_scalar(T.mkf[:, 4:8], T.mki[:], 0.0, -2048.0, A.is_equal, A.mult).then_inc(sem.vm, 1)
     V.wait_ge(sem.dl, 32)
     V.wait_ge(sem.arr, 7 * neng)
-    for x in range(2):
-        V.tensor_copy(T["l%d" % x][:], T.land[:, 4 * x:4 * x + 4, 0:16]).then_inc(sem["cp%d" % x], 1)
-    V.wait_ge(sem.vm, 4)
-    prep(0)
-    prep(1)
-    V.wait_ge(sem.dw, 64)
-    S.wait_ge(sem.vm, 4)
-    S.wait_ge(sem.dw, 64)
-    pieces(UP[1])
-    P.wait_ge(sem.vk, 7)
+    bits(T.pxy[:, 1, :, :], T.land[:, :, 16:32], 0, 4095).then_inc(sem.vp, 1)
+    bits(T.pxy[:, 0, :, :], T.land[:, :, 16:32], 12, 0).then_inc(sem.vp, 1)
+    V.tensor_copy(T.lst[:], T.land[:, :, 0:16]).then_inc(sem.l0, 1)
+    V.wait_ge(sem.vm, 2)
+    V.wait_ge(sem.vp, 2)
+    for h in range(4):
+        V.tensor_scalar(T.cx[:, 0, :, h:64:4], T.pxy[:, 0, :, :], -2048.0, T.mkf[:, h:h + 1], A.add, A.mult).then_inc(sem.vx, 1)
 
-    for i in range(R):
-        vg(0, i, 0, VM)
+    out(S, PRE_S)
+    S.wait_ge(sem.gq, 4)
+    S.activation(T.qz[:, :, 2], T.qz[:, :, 3], F.Copy, scale=-1.0).then_inc(sem.sn, 1)
+    S.wait_ge(sem.vm, 2)
+    S.wait_ge(sem.vp, 1)
+    for h in range(4):
+        S.activation(T.cx[:, 1, :, h:64:4], T.pxy[:, 1, :, :], F.Identity, bias=T.mkf[:, 4 + h:5 + h],
+                     scale=T.mkf[:, h:h + 1]).then_inc(sem.sx, 1)
+    for q in (V, S):
+        q.wait_ge(sem.l0, 1)
+        q.wait_ge(sem.dw, 64)
+
+    ngs, ngv, nfu = [0] * NB, [0] * NB, [0] * NB
+
+    def gather(q, n, c0, c1):
+        x, i = n % NB, n // NB
+        if c0 >= c1:
+            return
         if i:
-            newlist(1, i - 1)
-        vg(0, i, VM, VW)
-        vg(1, i, 0, VW)
-        out(UP[i + 1])
-        newlist(0, i)
-        sg(0, i)
-        sg(1, i)
-        absolute(0, i)
-        absolute(1, i)
-        if i == 0:
-            for x in range(2):
-                P.wait_ge(sem["vp%d" % x], 7)
-                places(x, 0)
-                times(x, 0)
-            rows(0, 0)
+            q.wait_ge(sem["cp%d" % x], i)
+        lst = T.lst[:, 32 * x + c0:32 * x + c1]
+        if i == R:
+            o, src = T.uo[:, 512 * x + 16 * c0:512 * x + 16 * c1], T.us[:, 0:L].indirect(lst)
+            own = 32 * x + c0 >= 16 * (N - 1)
+            (V.tensor_copy(o, src) if q is V else S.activation(o, src, F.Copy)).then_inc(sem.fo if own else sem["fu%d" % x], 1)
+            nfu[x] += not own
+        elif q is V:
+            V.tensor_scalar(T["v%d" % x][:, 16 * c0:16 * c1], T.win[:, 0:L].indirect(lst), -2048.0, None, A.add).then_inc(sem["gv%d" % x], 1)
+            ngv[x] += 1
         else:
-            rows(0, i)
-            times(1, i)
-        rows(1, i)
-        back(0, i)
-        back(1, i)
-        if i < R - 1:
-            places(0, i + 1)
-            places(1, i + 1)
-            pieces(UP[i + 2])
-            times(0, i + 1)
+            S.activation(T["v%d" % x][:, 16 * c0:16 * c1], T.win[:, 0:L].indirect(lst), F.Copy, bias=-2048.0).then_inc(sem["gs%d" % x], 1)
+            ngs[x] += 1
 
-    def final(x, q, c0, c1):
-        o, src = T["u%d" % x][:, 16 * c0:16 * c1], T.us[:, 0:L].indirect(T["l%d" % x][:, c0:c1])
-        if q is V:
-            V.tensor_copy(o, src).then_inc(sem["fv%d" % x], 1)
-        else:
-            S.activation(o, src, F.Copy).then_inc(sem["fs%d" % x], 1)
+    def places(n):
+        x, i = n % NB, n // NB
+        if i:
+            P.wait_ge(sem["cp%d" % x], i)
+        for c in range(2):
+            P.matmul(T["p%d" % x][:, 0:8, :, :], T.cx[:, c, 2 * x:2 * x + 2, :], T.qz[:, :, 2 - 2 * c:6 - 2 * c], c == 0,
+                     False).then_inc(sem["st%d" % x], 1)
 
-    for q in (S, V):
-        q.wait_ge(sem.ga0, 16)
-        q.wait_ge(sem.ga1, 16)
-        q.wait_ge(sem.vu, sum(UP))
-        q.wait_ge(sem.cp0, R + 1)
-    final(0, V, 0, VF)
-    final(0, S, VF, 64)
-    newlist(1, R - 1)
-    V.wait_ge(sem.cp1, R + 1)
-    S.wait_ge(sem.cp1, R + 1)
-    final(1, V, 0, 16)
-    final(1, S, 16, 32)
-    final(1, V, 32, 40)
-    final(1, S, 40, 48)
-    final(1, V, 48, 56)
-    final(1, S, 56, 64)
+    def rows(n):
+        x = n % NB
+        P.wait_ge(sem["gv%d" % x], ngv[x])
+        P.wait_ge(sem["gs%d" % x], ngs[x])
+        for b in range(4):
+            P.matmul(T["p%d" % x][:, 0:8, b, :], T["v%d" % x][:, b:512:4], T.r32[:], False, b == 3).then_inc(sem["st%d" % x], 1)
+
+    def largest(n):
+        x, i = n % NB, n // NB
+        V.wait_ge(sem["st%d" % x], 6 * (i + 1))
+        V.tensor_reduce(T.a[:, 36 * x + 3:36 * x + 32:4, :], T["p%d" % x][:, 0:8, :, :], AxisListType.X, A.max).then_inc(sem["ab%d" % x], 1)
+
+    def back(n):
+        x, i = n % NB, n // NB
+        P.wait_ge(sem["ab%d" % x], i + 1)
+        for h in range(4):
+            P.matmul(T["p%d" % x][:, 16:18, :, :], T.a[:, 36 * x + 3 - h:36 * x + 35 - h, :], T.rb[:, h, :], h == 0,
+                     h == 3).then_inc(sem["tr%d" % x], 1)
+
+    def newlist(n):
+        x, i = n % NB, n // NB
+        V.wait_ge(sem["tr%d" % x], 4 * (i + 1))
+        V.tensor_tensor(T.lst[:, 32 * x:32 * x + 32], T["p%d" % x][:, 16:18, :, :], T.land[:, 2 * x:2 * x + 2, 0:16],
+                        A.add).then_inc(sem["cp%d" % x], 1)
+
+    P.wait_ge(sem.vx, 4)
+    P.wait_ge(sem.sx, 4)
+    P.wait_ge(sem.sn, 1)
+    for n in range(LEAD):
+        places(n)
+    P.wait_ge(sem.ge, 3)
+    P.wait_ge(sem.gm, 1)
+    P.wait_ge(sem.za, 3)
+
+    last = NB * R
+    for n in range(last + NB):
+        x, i = n % NB, n // NB
+        nc = 32 - 16 * (n == last + NB - 1)
+        w = (VW0 if i == 0 else VF if i == R else VW)[x]
+        if n == last:
+            for q in (S, V, P):
+                for s in nout:
+                    if nout[s]:
+                        q.wait_ge(sem[s], nout[s])
+            for q in (S, V):
+                q.wait_ge(sem.ga0, 16)
+                q.wait_ge(sem.ga1, 16)
+        steps = {"r": lambda: largest(n - LAGR) if 0 <= n - LAGR < last else None,
+                 "l": lambda: newlist(n - LAGN) if 0 <= n - LAGN < last else None,
+                 "g": lambda: gather(V, n, 0, min(w, nc))}
+        for k in ("rlg", "rgl", "grl", "lrg", "glr", "lgr")[VO]:
+            steps[k]()
+        gather(S, n, min(w, nc), nc)
+        if n < last:
+            out(V, IN_V[n])
+            out(S, IN_S[n])
+        steps = {"b": lambda: back(n - LAGB) if 0 <= n - LAGB < last else None,
+                 "r": lambda: rows(n) if n < last else None,
+                 "p": lambda: places(n + LEAD) if n + LEAD < last else None}
+        for k in ("brp", "bpr", "rbp", "rpb", "pbr", "prb")[PO]:
+            steps[k]()
+        piece()
+    gather(V, last + NB - 1, 16, 24)
+    gather(S, last + NB - 1, 24, 32)
 
     nloc = 0
-    for j, slots in enumerate(CALLS):
-        x = slots[0] // 4
-        g.wait_ge(sem["fv%d" % x], max(j, 1))
-        g.wait_ge(sem["fs%d" % x], max(j, 1))
+    for x in range(NB):
+        slots = range(2 * x, min(2 * x + 2, N - 1))
+        g.wait_ge(sem["fu%d" % x], nfu[x])
         tr = []
         for k, s in enumerate(slots):
             d = T.cores[(me + 1 + s) % N]
             rid, pid, _ = topo.addr(d)
             e = topo.engines(core, d)
-            w = len(e) // WIDTH[s]
+            w = len(e) // len(slots)
             tr.append(RemoteDMATransfer(dst_ids=[DstId(rid=rid, pnc=pid)], dma_engine_mask=sum(1 << m for m in e[w * k:w * k + w]),
-                                        remote_sem=sem["uq%d" % me], srcs=[T["u%d" % x][:, 256 * (s % 4):256 * (s % 4) + 256]],
-                                        dsts=[T.ul[:, me, :]]))
+                                        remote_sem=sem["uq%d" % me], srcs=[T.uo[:, 256 * s:256 * s + 256]], dsts=[T.ul[:, me, :]]))
             nloc += w
         g.remote_dma_fused(tr, local_sem=sem.lu)
 
-    P.wait_ge(sem.vu, sum(UP))
     for q in range(N):
         if q == me:
-            P.wait_ge(sem.fv1, 3)
-            P.wait_ge(sem.fs1, 3)
+            P.wait_ge(sem.fo, 2)
         else:
-            P.wait_ge(sem["uq%d" % q], len(topo.engines(T.cores[q], core)) // WIDTH[(me - q - 1) % N])
+            P.wait_ge(sem["uq%d" % q], len(topo.engines(T.cores[q], core)) // (1 if (me - q - 1) % N == N - 2 else 2))
         for h in range(2):
-            src = T.u1[:, 768 + 128 * h:896 + 128 * h] if q == me else T.ul[:, q, 128 * h:128 * h + 128]
+            src = T.uo[:, 1792 + 128 * h:1920 + 128 * h] if q == me else T.ul[:, q, 128 * h:128 * h + 128]
             P.matmul(T["w%d" % h][:, 0:128], T.i1[:], src, q == 0, q == N - 1).then_inc(sem["yp%d" % h], 1)
     V.wait_ge(sem.yp0, N)
     V.tensor_copy(T.ysb[:, 0:128], T.w0[:, 0:128]).then_inc(sem.yc0, 1)

from concourse.bass import DstId, RemoteDMATransfer
from concourse.mybir import AluOpType, ActivationFunctionType, AxisListType

N = 8
R = 5
L = 8192
REG = 4096
ZA = 2304
ZV = 5632
ZG, Z0, ZS = 7680, 384, 1024
NB = 4
VW = (14, 14, 14, 14)
VW0 = (18, 20, 12, 14)
VF = (12, 14, 12, 10)
LAGR = 2
LAGN = 3
VO = 0
LAGB = 1
LEAD = 1
PO = 2
PW = 256
NW = 4
PRE_S, PRE_V = 2, 0
IN_S = [0, 1, 1, 0, 1, 0, 1, 0, 1, 0, 0, 0, 1, 0, 0, 0, 1, 0, 0, 0]
IN_V = [0, 0, 0, 0, 0, 0, 0, 0, 0, 0, 0, 0, 0, 0, 0, 0, 0, 0, 0, 0]
NP = PRE_S + PRE_V + sum(IN_S) + sum(IN_V)
H = PW * NP
CUTS = [0, 1040, 1040, H + 16]
MID = 5632
SCRATCH = {
    "land": ("sbuf", [128, 8, 32], "int32"),
    "pxy": ("sbuf", [128, 2, 8, 16], "int32"),
    "cx": ("sbuf", [128, 2, 8, 64], "float16"),
    "win": ("sbuf", [128, L], "int32"),
    "snd": ("sbuf", [128, H + 16], "bfloat16"),
    "us": ("sbuf", [128, L], "bfloat16"),
    "trk": ("sbuf", [128, 512], "int32"),
    "dig": ("sbuf", [128, 2, 512], "int32"),
    "uo": ("sbuf", [128, 2048], "bfloat16"),
    "ul": ("sbuf", [128, 8, 256], "bfloat16"),
    "ysb": ("sbuf", [128, 256], "float32"),
    "zb": ("sbuf", [128, 192], "bfloat16"),
    "i1": ("sbuf", [128, 128], "bfloat16"),
    "r32": ("sbuf", [128, 8, 4], "bfloat16"),
    "qz": ("sbuf", [128, 32, 6], "bfloat16"),
    "rb": ("sbuf", [128, 4, 32], "bfloat16"),
    "pi": ("sbuf", [128, 4], "int32"),
    "mki": ("sbuf", [128, 4], "int32"),
    "mkf": ("sbuf", [128, 8], "float32"),
    "lst": ("sbuf", [128, 128], "uint16"),
    "a": ("sbuf", [128, 36 * NB, 4], "float16"),
}
for _x in range(NB):
    SCRATCH["v%d" % _x] = ("sbuf", [128, 512], "float16")
    SCRATCH["p%d" % _x] = ("psum", [128, 32, 4, 4], "float32")
for _x in range(NW):
    SCRATCH["w%d" % _x] = ("psum", [128, 512], "float32")
SEMAPHORES = (["vz", "vy", "gi", "gz", "ge", "gq", "gm", "g1", "vb", "vm", "dl", "dt", "vp", "vx", "sx", "sn", "sz", "dw", "vd0", "vd1",
               "arr", "ls", "lu", "yp0", "yp1", "yc0", "yc1", "dy0", "dy1", "ds0", "ds1", "ds2", "dn1", "dn3", "ga0", "ga1",
               "pu", "ov", "ow", "vw", "sy", "fo", "l0", "za"]
              + ["%s%d" % (k, x) for k in ("gv", "gs", "st", "ab", "tr", "cp", "fu") for x in range(NB)]
              + ["uq%d" % q for q in range(N)])


def rank_program(g, core, T, topo):
    me = T.rank_of(core)
    if me is None:
        return
    A, F = AluOpType, ActivationFunctionType
    V, S, P, Y = g.vector, g.scalar, g.tensor, g.sync
    sem = T.sem
    AND, SHR = A.bitwise_and, A.logical_shift_right

    def bits(out, in_, shift, mask):
        if shift and mask:
            return V.tensor_scalar(out, in_, shift, mask, SHR, AND)
        if shift:
            return V.tensor_scalar(out, in_, shift, None, SHR)
        return V.tensor_scalar(out, in_, mask, None, AND)

    def sound(k):
        if CUTS[k] < CUTS[k + 1]:
            Y.dma_start(T.snd[:, CUTS[k]:CUTS[k + 1]], T.sound[:, CUTS[k]:CUTS[k + 1]]).then_inc(sem["ds%d" % k], 16)

    S.dma_start(T.land[:, 7, 16:32], T.place[:]).then_inc(sem.dl, 16)
    Y.dma_start(T.land[:, 7, 0:16], T.when[:]).then_inc(sem.dl, 16)
    Y.dma_start(T.trk[:, 0:REG // 16], T.track[:, 0:REG]).then_inc(sem.dt, 16)
    S.dma_start(T.trk[:, REG // 16:512], T.track[:, REG:L]).then_inc(sem.dt, 16)
    sound(0)
    sound(1)

    V.memset(T.win[:, 0:Z0], 0).then_inc(sem.vy, 1)
    V.memset(T.zb[:], 0.0).then_inc(sem.vz, 1)
    V.memset(T.win[:, Z0:ZS], 0).then_inc(sem.vy, 1)
    V.memset(T.win[:, ZS:ZA], 0).then_inc(sem.vy, 1)
    S.wait_ge(sem.vy, 1)
    S.activation(T.win[:, ZA:ZA + Z0], T.win[:, 0:Z0], F.Copy).then_inc(sem.sz, 1)
    S.wait_ge(sem.vy, 2)
    nz = [1, 1]
    for k in range(ZA + Z0, REG, ZS):
        w = min(ZS, REG - k)
        S.activation(T.win[:, k:k + w], T.win[:, 0:w], F.Copy).then_inc(sem.sz, 1)
        nz[0] += 1
    z1 = 2 * ZG - L
    S.wait_ge(sem.gz, 1)
    S.activation(T.win[:, z1:ZG], T.win[:, ZG:L], F.Copy).then_inc(sem.sy, 1)
    for k in range(ZV, z1, L - ZG):
        w = min(L - ZG, z1 - k)
        S.activation(T.win[:, k:k + w], T.win[:, ZG:ZG + w], F.Copy).then_inc(sem.sy, 1)
        nz[1] += 1

    g.iota(T.win[:, ZG:L], [[0, L - ZG]], 0, 0).then_inc(sem.gz, 1)
    others = [(me + d) % N for d in range(1, N)]
    dst0 = T.cores[others[0]]
    mask = topo.mask(core, dst0)
    neng = len(topo.engines(core, dst0))
    ids, dsts = [], []
    for r in others:
        rid, pid, _ = topo.addr(T.cores[r])
        ids.append(DstId(rid=rid, pnc=pid))
        dsts.append(T.land[:, (me - r - 1) % N, :])
    g.wait_ge(sem.dl, 32)
    g.remote_dma_fused([RemoteDMATransfer(dst_ids=ids, dma_engine_mask=mask, remote_sem=sem.arr, srcs=[T.land[:, 7, :]], dsts=dsts)],
                       local_sem=sem.ls)
    g.wait_ge(sem.vz, 1)
    g.affine_select(T.i1[:], T.zb[:, 0:128], [[-1, 128]], A.not_equal, 1.0, 0, 1).then_inc(sem.g1, 1)
    g.iota(T.pi[:], [[-4, 4]], 16, 1).then_inc(sem.gi, 1)
    g.affine_select(T.qz[:], T.zb[:], [[-16, 8], [-1, 4], [128, 6]], A.not_equal, 1.0, -384, 1).then_inc(sem.gq, 1)
    g.affine_select(T.r32[:], T.zb[:, 0:32], [[-16, 8], [0, 4]], A.not_equal, 1.0, -2, 1).then_inc(sem.ge, 1)
    for h in range(1, 4):
        g.wait_ge(sem.gq, h)
        g.affine_select(T.qz[:, :, 3], T.qz[:, :, 3], [[-16, 8], [-1, 4]], A.not_equal, 1.0, -4 * h, 1).then_inc(sem.gq, 1)
        if h < 3:
            g.wait_ge(sem.ge, 1)
            g.affine_select(T.r32[:, :, h - 1:4:2], T.r32[:, :, h - 1:4:2], [[-16, 8], [-1, 2]], A.not_equal, 3.0 - 2 * h, 0, 1).then_inc(sem.ge, 1)
    g.affine_select(T.rb[:], T.zb[:, 0:128], [[-1, 4], [-4, 32]], A.not_equal, -1.0, 0, 1).then_inc(sem.gm, 1)

    V.wait_ge(sem.dt, 32)
    bits(T.dig[:, 0, :], T.trk[:], 12, 0).then_inc(sem.vd0, 1)
    bits(T.dig[:, 1, :], T.trk[:], 0, 4095).then_inc(sem.vd1, 1)
    V.memset(T.win[:, REG:ZV], 0).then_inc(sem.vw, 1)
    Y.wait_ge(sem.vy, 3)
    Y.wait_ge(sem.sz, nz[0])
    for c in range(2):
        Y.wait_ge(sem["vd%d" % c], 1)
        Y.dma_start(T.win[c:128:16, 0:REG], T.dig[:, c, 0:REG // 16]).then_inc(sem.dw, 16)
    Y.wait_ge(sem.vw, 1)
    Y.wait_ge(sem.sy, nz[1])
    Y.wait_ge(sem.gz, 1)
    for c in range(2):
        Y.dma_start(T.win[c:128:16, REG:L], T.dig[:, c, REG // 16:512]).then_inc(sem.dw, 16)
    sound(2)
    Y.dma_start(T.us[:, H:MID], T.sound[:, H:MID]).then_inc(sem.dn1, 16)
    Y.dma_start(T.us[:, MID:L], T.sound[:, MID:L]).then_inc(sem.dn3, 16)
    g.wait_ge(sem.dn1, 16)
    g.dma_start(T.us[:, H:MID], T.sound[:, H + 1:MID + 1], accum_op=A.add, max_dma_last_dim=4096).then_inc(sem.ga0, 16)
    g.wait_ge(sem.dn3, 16)
    g.dma_start(T.us[:, MID:L - 1], T.sound[:, MID + 1:L], accum_op=A.add, max_dma_last_dim=4096).then_inc(sem.ga1, 16)

    made, outs, loaded = [0], [], [0]

    def piece(early=False):
        k = made[0]
        if k >= NP or k - NW >= len(outs) or (early and PW * k + PW + 1 > CUTS[2]):
            return
        if k == 0:
            P.wait_ge(sem.g1, 1)
        while CUTS[loaded[0]] < PW * k + PW + 1:
            if CUTS[loaded[0]] < CUTS[loaded[0] + 1]:
                P.wait_ge(sem["ds%d" % loaded[0]], 16)
            loaded[0] += 1
        if k >= NW:
            P.wait_ge(*outs[k - NW])
        w = T["w%d" % (k % NW)][:, 0:PW]
        P.matmul(w, T.i1[:], T.snd[:, PW * k:PW * k + PW], True, False).then_inc(sem.pu, 1)
        P.matmul(w, T.i1[:], T.snd[:, PW * k + 1:PW * k + PW + 1], False, True).then_inc(sem.pu, 1)
        made[0] += 1

    nout = {"ov": 0, "ow": 0}

    def out(q, n):
        for _ in range(n):
            k = len(outs)
            q.wait_ge(sem.pu, 2 * k + 2)
            o, w = T.us[:, PW * k:PW * k + PW], T["w%d" % (k % NW)][:, 0:PW]
            s = "ov" if q is V else "ow"
            (V.tensor_copy(o, w) if q is V else S.activation(o, w, F.Copy)).then_inc(sem[s], 1)
            nout[s] += 1
            outs.append((sem[s], nout[s]))

    for _ in range(NW):
        piece(True)

    V.wait_ge(sem.gi, 1)
    bits(T.mki[:], T.pi[:], 2, 3).then_inc(sem.vb, 1)
    for k in range(3):
        V.memset(T.a[:, k:36 * NB:4, :], 0.0 if k else 2048.0).then_inc(sem.za, 1)
    out(V, PRE_V)
    V.wait_ge(sem.vb, 1)
    V.tensor_scalar(T.mkf[:, 0:4], T.mki[:], 0.0, None, A.is_equal).then_inc(sem.vm, 1)
    V.tensor_scalar(T.mkf[:, 4:8], T.mki[:], 0.0, -2048.0, A.is_equal, A.mult).then_inc(sem.vm, 1)
    V.wait_ge(sem.dl, 32)
    V.wait_ge(sem.arr, 7 * neng)
    bits(T.pxy[:, 1, :, :], T.land[:, :, 16:32], 0, 4095).then_inc(sem.vp, 1)
    bits(T.pxy[:, 0, :, :], T.land[:, :, 16:32], 12, 0).then_inc(sem.vp, 1)
    V.tensor_copy(T.lst[:], T.land[:, :, 0:16]).then_inc(sem.l0, 1)
    V.wait_ge(sem.vm, 2)
    V.wait_ge(sem.vp, 2)
    for h in range(4):
        V.tensor_scalar(T.cx[:, 0, :, h:64:4], T.pxy[:, 0, :, :], -2048.0, T.mkf[:, h:h + 1], A.add, A.mult).then_inc(sem.vx, 1)

    out(S, PRE_S)
    S.wait_ge(sem.gq, 4)
    S.activation(T.qz[:, :, 2], T.qz[:, :, 3], F.Copy, scale=-1.0).then_inc(sem.sn, 1)
    S.wait_ge(sem.vm, 2)
    S.wait_ge(sem.vp, 1)
    for h in range(4):
        S.activation(T.cx[:, 1, :, h:64:4], T.pxy[:, 1, :, :], F.Identity, bias=T.mkf[:, 4 + h:5 + h],
                     scale=T.mkf[:, h:h + 1]).then_inc(sem.sx, 1)
    for q in (V, S):
        q.wait_ge(sem.l0, 1)
        q.wait_ge(sem.dw, 64)

    ngs, ngv, nfu = [0] * NB, [0] * NB, [0] * NB

    def gather(q, n, c0, c1):
        x, i = n % NB, n // NB
        if c0 >= c1:
            return
        if i:
            q.wait_ge(sem["cp%d" % x], i)
        lst = T.lst[:, 32 * x + c0:32 * x + c1]
        if i == R:
            o, src = T.uo[:, 512 * x + 16 * c0:512 * x + 16 * c1], T.us[:, 0:L].indirect(lst)
            own = 32 * x + c0 >= 16 * (N - 1)
            (V.tensor_copy(o, src) if q is V else S.activation(o, src, F.Copy)).then_inc(sem.fo if own else sem["fu%d" % x], 1)
            nfu[x] += not own
        elif q is V:
            V.tensor_scalar(T["v%d" % x][:, 16 * c0:16 * c1], T.win[:, 0:L].indirect(lst), -2048.0, None, A.add).then_inc(sem["gv%d" % x], 1)
            ngv[x] += 1
        else:
            S.activation(T["v%d" % x][:, 16 * c0:16 * c1], T.win[:, 0:L].indirect(lst), F.Copy, bias=-2048.0).then_inc(sem["gs%d" % x], 1)
            ngs[x] += 1

    def places(n):
        x, i = n % NB, n // NB
        if i:
            P.wait_ge(sem["cp%d" % x], i)
        for c in range(2):
            P.matmul(T["p%d" % x][:, 0:8, :, :], T.cx[:, c, 2 * x:2 * x + 2, :], T.qz[:, :, 2 - 2 * c:6 - 2 * c], c == 0,
                     False).then_inc(sem["st%d" % x], 1)

    def rows(n):
        x = n % NB
        P.wait_ge(sem["gv%d" % x], ngv[x])
        P.wait_ge(sem["gs%d" % x], ngs[x])
        for b in range(4):
            P.matmul(T["p%d" % x][:, 0:8, b, :], T["v%d" % x][:, b:512:4], T.r32[:], False, b == 3).then_inc(sem["st%d" % x], 1)

    def largest(n):
        x, i = n % NB, n // NB
        V.wait_ge(sem["st%d" % x], 6 * (i + 1))
        V.tensor_reduce(T.a[:, 36 * x + 3:36 * x + 32:4, :], T["p%d" % x][:, 0:8, :, :], AxisListType.X, A.max).then_inc(sem["ab%d" % x], 1)

    def back(n):
        x, i = n % NB, n // NB
        P.wait_ge(sem["ab%d" % x], i + 1)
        for h in range(4):
            P.matmul(T["p%d" % x][:, 16:18, :, :], T.a[:, 36 * x + 3 - h:36 * x + 35 - h, :], T.rb[:, h, :], h == 0,
                     h == 3).then_inc(sem["tr%d" % x], 1)

    def newlist(n):
        x, i = n % NB, n // NB
        V.wait_ge(sem["tr%d" % x], 4 * (i + 1))
        V.tensor_tensor(T.lst[:, 32 * x:32 * x + 32], T["p%d" % x][:, 16:18, :, :], T.land[:, 2 * x:2 * x + 2, 0:16],
                        A.add).then_inc(sem["cp%d" % x], 1)

    P.wait_ge(sem.vx, 4)
    P.wait_ge(sem.sx, 4)
    P.wait_ge(sem.sn, 1)
    for n in range(LEAD):
        places(n)
    P.wait_ge(sem.ge, 3)
    P.wait_ge(sem.gm, 1)
    P.wait_ge(sem.za, 3)

    last = NB * R
    for n in range(last + NB):
        x, i = n % NB, n // NB
        nc = 32 - 16 * (n == last + NB - 1)
        w = (VW0 if i == 0 else VF if i == R else VW)[x]
        if n == last:
            for q in (S, V, P):
                for s in nout:
                    if nout[s]:
                        q.wait_ge(sem[s], nout[s])
            for q in (S, V):
                q.wait_ge(sem.ga0, 16)
                q.wait_ge(sem.ga1, 16)
        steps = {"r": lambda: largest(n - LAGR) if 0 <= n - LAGR < last else None,
                 "l": lambda: newlist(n - LAGN) if 0 <= n - LAGN < last else None,
                 "g": lambda: gather(V, n, 0, min(w, nc))}
        for k in ("rlg", "rgl", "grl", "lrg", "glr", "lgr")[VO]:
            steps[k]()
        gather(S, n, min(w, nc), nc)
        if n < last:
            out(V, IN_V[n])
            out(S, IN_S[n])
        steps = {"b": lambda: back(n - LAGB) if 0 <= n - LAGB < last else None,
                 "r": lambda: rows(n) if n < last else None,
                 "p": lambda: places(n + LEAD) if n + LEAD < last else None}
        for k in ("brp", "bpr", "rbp", "rpb", "pbr", "prb")[PO]:
            steps[k]()
        piece()
    gather(V, last + NB - 1, 16, 24)
    gather(S, last + NB - 1, 24, 32)

    nloc = 0
    for x in range(NB):
        slots = range(2 * x, min(2 * x + 2, N - 1))
        g.wait_ge(sem["fu%d" % x], nfu[x])
        tr = []
        for k, s in enumerate(slots):
            d = T.cores[(me + 1 + s) % N]
            rid, pid, _ = topo.addr(d)
            e = topo.engines(core, d)
            w = len(e) // len(slots)
            tr.append(RemoteDMATransfer(dst_ids=[DstId(rid=rid, pnc=pid)], dma_engine_mask=sum(1 << m for m in e[w * k:w * k + w]),
                                        remote_sem=sem["uq%d" % me], srcs=[T.uo[:, 256 * s:256 * s + 256]], dsts=[T.ul[:, me, :]]))
            nloc += w
        g.remote_dma_fused(tr, local_sem=sem.lu)

    for q in range(N):
        if q == me:
            P.wait_ge(sem.fo, 2)
        else:
            P.wait_ge(sem["uq%d" % q], len(topo.engines(T.cores[q], core)) // (1 if (me - q - 1) % N == N - 2 else 2))
        for h in range(2):
            src = T.uo[:, 1792 + 128 * h:1920 + 128 * h] if q == me else T.ul[:, q, 128 * h:128 * h + 128]
            P.matmul(T["w%d" % h][:, 0:128], T.i1[:], src, q == 0, q == N - 1).then_inc(sem["yp%d" % h], 1)
    V.wait_ge(sem.yp0, N)
    V.tensor_copy(T.ysb[:, 0:128], T.w0[:, 0:128]).then_inc(sem.yc0, 1)
    Y.wait_ge(sem.yc0, 1)
    Y.dma_start(T.y[:, 0:128], T.ysb[:, 0:128]).then_inc(sem.dy0, 16)
    Y.wait_ge(sem.dy0, 16)
    S.wait_ge(sem.yp1, N)
    S.activation(T.ysb[:, 128:256], T.w1[:, 0:128], F.Copy).then_inc(sem.yc1, 1)
    S.wait_ge(sem.yc1, 1)
    S.dma_start(T.y[:, 128:256], T.ysb[:, 128:256]).then_inc(sem.dy1, 16)
    S.wait_ge(sem.dy1, 16)
    g.wait_ge(sem.ls, neng)
    g.wait_ge(sem.lu, nloc)
